import numpy as np
import ml_dtypes


def mxq(x, axis, fmt="e4m3"):
    dtype, down = {"e4m3": (ml_dtypes.float8_e4m3fn, 7), "e5m2": (ml_dtypes.float8_e5m2, 14)}[fmt]
    v = np.moveaxis(np.asarray(x, np.float32).astype(ml_dtypes.bfloat16).astype(np.float64), axis, -1)
    blocks = v.reshape(v.shape[:-1] + (-1, 32))
    amax = np.abs(blocks).max(-1, keepdims=True)
    byte = np.maximum(np.where(amax > 0, np.frexp(amax)[1] - 1 + 127, 0) - down, 1)
    scale = np.exp2(byte - 127.0)
    codes = (blocks / scale).astype(np.float32).astype(dtype).astype(np.float64)
    return np.moveaxis((codes * scale).reshape(v.shape), -1, axis)


WIDE = False


def mx_kscale(k):
    if not WIDE:
        return np.ones(k)
    levels = np.array([10, -10, 5, -5, 0])
    if k % 512:
        return np.exp2(np.random.permutation(np.resize(levels, k // 32))).repeat(32)
    a = np.empty((k // 512, 16))
    for p in range(k // 512):
        a[p, :8] = np.random.permutation(np.resize(levels, 8))
        for g in range(8):
            far = levels[np.abs(levels - a[p, g]) >= 10]
            a[p, g + 8] = far[np.random.randint(len(far))]
    return np.exp2(a.ravel()).repeat(32)


def f64(x):
    return np.asarray(x).astype(np.float64)


def striped(idx):
    return np.tile(np.asarray(idx).reshape(-1, 16).T, (8, 1)).astype(np.uint16)


def unstriped(offs):
    return offs[:16].T.reshape(-1).astype(np.int64)


E2M1 = np.array([0.0, 0.5, 1.0, 1.5, 2.0, 3.0, 4.0, 6.0, -0.0, -0.5, -1.0, -1.5, -2.0, -3.0, -4.0, -6.0])


def pack_weight(w, fmt):
    k, n = w.shape
    w = f64(np.asarray(w, np.float32).astype(ml_dtypes.bfloat16)).reshape(k // 32, 32, n)
    amax = np.abs(w).max(1)
    if fmt == "e4m3":
        byte = np.frexp(amax)[1] - 1 + 127 - 7
    else:
        mant, ex = np.frexp(amax / 6.0)
        byte = np.where(mant > 0.5, ex, ex - 1) + 127
    byte = np.clip(np.where(amax > 0, byte, 1), 1, 254)
    scaled = (w * np.exp2(127.0 - byte)[:, None, :]).reshape(k, n).astype(np.float32)
    by_word = np.ascontiguousarray(scaled.reshape(k // 512, 128, 4, n).transpose(0, 1, 3, 2))
    if fmt == "e4m3":
        words = by_word.astype(ml_dtypes.float8_e4m3fn).view(np.uint8)
    else:
        c = by_word.astype(ml_dtypes.float4_e2m1fn).view(np.uint8) & 0xF
        words = (c[..., 0::2] | (c[..., 1::2] << 4)).reshape(k // 512, 128, 2 * n)
    return np.ascontiguousarray(words), np.ascontiguousarray(byte.astype(np.uint8).reshape(k // 512, 16, n))


def unpack_weight(words, scales, fmt):
    g, _, n = scales.shape
    words = np.ascontiguousarray(words).reshape(g, 128, n, -1)
    if fmt == "e4m3":
        vals = words.view(ml_dtypes.float8_e4m3fn).astype(np.float64)
    else:
        nib = np.empty((g, 128, n, 4), np.uint8)
        nib[..., 0::2] = words & 0xF
        nib[..., 1::2] = words >> 4
        vals = E2M1[nib]
    vals = vals * np.repeat(np.exp2(scales.astype(np.float64) - 127.0), 8, axis=1)[..., None]
    return vals.transpose(0, 1, 3, 2).reshape(g * 512, n)


K, T, J, B, R, N = 512, 1024, 512, 64, 512, 512


def setup_inputs():
    n = np.random.standard_normal
    idx = (np.random.permutation(T // 8)[:J // 8, None] * 8 + np.arange(8)).reshape(-1)
    fk = mx_kscale(K)
    fr = mx_kscale(R)
    xtp = pack_weight(n((K, T)) / fk[:, None], "e4m3")
    wap = pack_weight(n((K, R)) * 1 / np.sqrt(K) * fk[:, None] * fr, "e2m1")
    wbp = pack_weight(n((R, N)) * 1 / np.sqrt(R) / fr[:, None], "e4m3")
    return {
        "xt_words": xtp[0],
        "xt_scales": xtp[1],
        "wa_words": wap[0],
        "wa_scales": wap[1],
        "wb_words": wbp[0],
        "wb_scales": wbp[1],
        "res": (1.0 * n((N, T))).astype(np.float32),
        "offs": striped(idx),
    }


def reference(xt_words, xt_scales, wa_words, wa_scales, wb_words, wb_scales, res, offs):
    idx = unstriped(offs)
    xtu = unpack_weight(xt_words, xt_scales, "e4m3")
    wau = unpack_weight(wa_words, wa_scales, "e2m1")
    wbu = unpack_weight(wb_words, wb_scales, "e4m3")
    xtidxg = xtu[:, idx]
    a = wau.T @ xtidxg
    m1 = a.reshape(R, B, J // B).mean(axis=2)
    mr = np.repeat(m1, J // B, axis=1)
    hid = np.maximum(a - mr, 0.0)
    hidq = mxq(hid, 0, "e4m3")
    p = wbu.T @ hidq
    pg = np.zeros((N, T))
    pg[:, idx] = p
    y = pg + 0.2 * f64(res)
    return y

@@ -1,0 +1,195 @@
+from contextlib import ExitStack
+
+import concourse.mybir as mybir
+
+K, T, J, R, N = 512, 1024, 512, 512, 512
+FLOPS = 2 * K * R * J + 2 * R * N * J
+
+F32 = mybir.dt.float32
+BF16 = mybir.dt.bfloat16
+I32 = mybir.dt.int32
+U32 = mybir.dt.uint32
+U16 = mybir.dt.uint16
+U8 = mybir.dt.uint8
+FP8X4 = mybir.dt.float8_e4m3fn_x4
+FP4X4 = mybir.dt.float4_e2m1fn_x4
+ALU = mybir.AluOpType
+ACT = mybir.ActivationFunctionType
+
+P = 128
+PACK = 4
+BLOCK = 8
+CHUNK = 128
+CHUNKS = J // CHUNK
+TILES = N // P
+
+
+def load_scale_rows(engine, plane, scales):
+    rows = scales[0].bitcast(I32).rearrange("(q r) c -> r q c", r=4)
+    for r in range(4):
+        engine.dma_start(out=plane[r:P:32, :].bitcast(I32), in_=rows[r])
+
+
+def tile_moe_expert_hidden_less_block_mean_kernel(
+    tc, xt_words, xt_scales, wa_words, wa_scales, wb_words, wb_scales, res, offs, out
+):
+    nc = tc.nc
+    with ExitStack() as ctx:
+        keep = ctx.enter_context(tc.tile_pool(name="keep", bufs=1))
+        psum = ctx.enter_context(tc.psum_pool(name="psum", bufs=1))
+
+        offsets = keep.tile([P, J // 16], U16, name="offsets")
+        x_plane = keep.tile([P, T], U8, name="x_plane", align_bytes=64)
+        wa_plane_raw = keep.tile([P, R], U8, name="wa_plane_raw", align_bytes=64)
+        wb_plane = keep.tile([P, N], U8, name="wb_plane", align_bytes=64)
+        x_codes = keep.tile([P, T], U32, name="x_codes", align_bytes=64)
+        wa_raw = keep.tile([P, 2 * R], U8, name="wa_raw", tag="wa_then_res", align_bytes=64)
+        wb_codes = keep.tile([P, N], U32, name="wb_codes", align_bytes=64)
+
+        nc.vector.memset(x_plane[:].bitcast(I32), 0)
+        nc.vector.memset(wa_plane_raw[:].bitcast(I32), 0)
+        nc.gpsimd.memset(wb_plane[:].bitcast(I32), 0)
+
+        nc.sync.dma_start(offsets[:], offs)
+        load_scale_rows(nc.sync, x_plane, xt_scales)
+        nc.sync.dma_start(out=wa_raw[:].bitcast(I32), in_=wa_words[0].bitcast(I32))
+        nc.sync.dma_start(out=x_codes[:].bitcast(I32), in_=xt_words[0].rearrange("p c r -> p (c r)").bitcast(I32))
+        load_scale_rows(nc.sync, wa_plane_raw, wa_scales)
+
+        windows = []
+        for w in range(2):
+            window = keep.tile([P, T], F32, name=f"window{w}")
+            nc.vector.memset(window[:], 0.0)
+            windows.append(window)
+
+        xg_plane = keep.tile([P, J], U8, name="xg_plane", align_bytes=64)
+        xg_codes = keep.tile([P, J], U32, name="xg_codes", align_bytes=64)
+        wa_codes = keep.tile([P, 2 * R], U8, name="wa_codes", align_bytes=64)
+        wa_plane = keep.tile([P, R], U8, name="wa_plane", align_bytes=64)
+
+        nc.vector.tensor_copy(out=xg_plane[:], in_=x_plane[:].indirect(offsets[:]))
+        nc.vector.tensor_copy(
+            out=wa_codes[:].bitcast(U16).rearrange("p (t c i) -> p c t i", t=PACK, i=8),
+            in_=wa_raw[:].bitcast(U16).rearrange("p (c i t) -> p c t i", t=PACK, i=8),
+        )
+        nc.vector.tensor_copy(out=xg_codes[:, :CHUNK], in_=x_codes[:].indirect(offsets[:, : CHUNK // 16]))
+        nc.vector.tensor_copy(
+            out=wa_plane[:].rearrange("p (t c i) -> p c t i", t=PACK, i=16),
+            in_=wa_plane_raw[:].rearrange("p (c i t) -> p c t i", t=PACK, i=16),
+        )
+        nc.vector.tensor_copy(out=xg_codes[:, CHUNK:], in_=x_codes[:].indirect(offsets[:, CHUNK // 16 :]))
+
+        residual = []
+        for n in range(TILES):
+            tag = "wa_then_res" if n == 0 else f"res{n}"
+            res_tile = keep.tile([P, T], F32, name=f"res{n}", tag=tag, align_bytes=64)
+            residual.append(res_tile)
+        nc.sync.dma_start(out=residual[0][:], in_=res[0:P, :])
+        nc.sync.dma_start(out=wb_codes[:].bitcast(I32), in_=wb_words[0].rearrange("p c r -> p (c r)").bitcast(I32))
+        load_scale_rows(nc.sync, wb_plane, wb_scales)
+        for n in range(1, TILES):
+            nc.sync.dma_start(out=residual[n][:], in_=res[n * P : (n + 1) * P, :])
+
+        pre = []
+        for c in range(CHUNKS):
+            bank = psum.tile([P, PACK * CHUNK], F32, name=f"pre{c}", tag=f"pre{c}")
+            slots = slice(c * CHUNK, (c + 1) * CHUNK)
+            for t in range(PACK):
+                nc.tensor.matmul_mx(
+                    out=bank[:, t * CHUNK : (t + 1) * CHUNK],
+                    lhsT=wa_codes[:, 2 * P * t : 2 * P * (t + 1)].bitcast(FP4X4),
+                    lhsT_scale=wa_plane[:, P * t : P * (t + 1)],
+                    rhs=xg_codes[:, slots].bitcast(FP8X4),
+                    rhs_scale=xg_plane[:, slots],
+                    start=True,
+                    stop=True,
+                )
+            pre.append(bank)
+
+        groups = PACK * CHUNK // BLOCK
+        answers = keep.tile([P, TILES * J], F32, name="answers")
+        sums, hidden = {}, {}
+
+        def block_sums(c):
+            sums[c] = keep.tile([P, groups], F32, name=f"sums{c}")
+            nc.vector.tensor_reduce(
+                out=sums[c][:], in_=pre[c][:].rearrange("p (g i) -> p g i", i=BLOCK), axis=mybir.AxisListType.X, op=ALU.add
+            )
+
+        def centre(c):
+            centred = keep.tile([P, PACK * CHUNK], F32, name=f"centred{c}")
+            nc.vector.scalar_tensor_tensor(
+                out=centred[:].rearrange("p (g i) -> p g i", i=BLOCK),
+                in0=sums[c][:].unsqueeze(2).to_broadcast([P, groups, BLOCK]),
+                scalar=-1.0 / BLOCK,
+                in1=pre[c][:].rearrange("p (g i) -> p g i", i=BLOCK),
+                op0=ALU.mult,
+                op1=ALU.add,
+            )
+            hidden[c] = keep.tile([P, CHUNK * PACK], BF16, name=f"hidden{c}", align_bytes=64)
+            nc.scalar.activation(
+                out=hidden[c][:].rearrange("p (c i t) -> p c t i", t=PACK, i=4),
+                in_=centred[:].rearrange("p (t c i) -> p c t i", t=PACK, i=4),
+                func=ACT.Relu,
+            )
+
+        def second_layer(c):
+            codes = keep.tile([P, CHUNK], U32, name=f"hid_codes{c}", align_bytes=64)
+            plane = keep.tile([P, CHUNK], U8, name=f"hid_plane{c}", align_bytes=64)
+            nc.vector.quantize_mx(out=codes[:].bitcast(FP8X4), scales=plane[:], in_=hidden[c][:])
+            parts = [(0, TILES, f"post{c}")] if c < CHUNKS - 1 else [(0, 1, f"post{c}"), (1, TILES, "pre0")]
+            for first, last, tag in parts:
+                bank = psum.tile([P, PACK * CHUNK], F32, name=f"post{c}_{first}", tag=tag)
+                for n in range(first, last):
+                    nc.tensor.matmul_mx(
+                        out=bank[:, n * CHUNK : (n + 1) * CHUNK],
+                        lhsT=wb_codes[:, n * P : (n + 1) * P].bitcast(FP8X4),
+                        lhsT_scale=wb_plane[:, n * P : (n + 1) * P],
+                        rhs=codes[:].bitcast(FP8X4),
+                        rhs_scale=plane[:],
+                        start=True,
+                        stop=True,
+                    )
+                nc.scalar.copy(
+                    out=answers[:].rearrange("p (n j) -> p n j", n=TILES)[:, first:last, c * CHUNK : (c + 1) * CHUNK],
+                    in_=bank[:].rearrange("p (n j) -> p n j", n=TILES)[:, first:last, :],
+                )
+
+        def scatter(n, first, last):
+            nc.vector.tensor_copy(
+                out=windows[n % 2][:].indirect(offsets[:, first // 16 : last // 16]),
+                in_=answers[:, n * J + first : n * J + last],
+            )
+
+        def finish(n, pieces):
+            width = T // pieces
+            for h in range(pieces):
+                cols = slice(h * width, (h + 1) * width)
+                result = keep.tile([P, width], F32, name=f"result{n}_{h}")
+                nc.vector.scalar_tensor_tensor(
+                    out=result[:], in0=residual[n][:, cols], scalar=0.2, in1=windows[n % 2][:, cols], op0=ALU.mult, op1=ALU.add
+                )
+                nc.sync.dma_start(out=out[n * P : (n + 1) * P, cols], in_=result[:])
+
+        block_sums(0)
+        block_sums(1)
+        centre(0)
+        block_sums(2)
+        centre(1)
+        block_sums(3)
+        second_layer(0)
+        centre(2)
+        second_layer(1)
+        centre(3)
+        second_layer(2)
+        scatter(0, 0, 2 * CHUNK)
+        second_layer(3)
+        scatter(1, 0, 3 * CHUNK)
+        scatter(0, 2 * CHUNK, J)
+        scatter(1, 3 * CHUNK, J)
+        finish(0, 1)
+        finish(1, 1)
+        scatter(2, 0, J)
+        scatter(3, 0, J)
+        finish(2, 1)
+        finish(3, 2)

@@ -1,6 +1,7 @@
 from contextlib import ExitStack
 
 import concourse.mybir as mybir
+from concourse.masks import make_identity
 
 K, T, J, R, N = 512, 1024, 512, 512, 512
 FLOPS = 2 * K * R * J + 2 * R * N * J
@@ -22,6 +23,9 @@ BLOCK = 8
 CHUNK = 128
 CHUNKS = J // CHUNK
 TILES = N // P
+BANK = 512
+TURNED_TILES = 2
+RES_SCALE = 0.2
 
 
 def load_scale_rows(engine, plane, scales):
@@ -40,67 +44,71 @@ def tile_moe_expert_hidden_less_block_mean_kernel(
 
         offsets = keep.tile([P, J // 16], U16, name="offsets")
         x_plane = keep.tile([P, T], U8, name="x_plane", align_bytes=64)
-        wa_plane_raw = keep.tile([P, R], U8, name="wa_plane_raw", align_bytes=64)
+        wa_plane_raw = keep.tile([P, R], U8, name="wa_plane_raw", tag="plane_then_codes", align_bytes=64)
         wb_plane = keep.tile([P, N], U8, name="wb_plane", align_bytes=64)
         x_codes = keep.tile([P, T], U32, name="x_codes", align_bytes=64)
-        wa_raw = keep.tile([P, 2 * R], U8, name="wa_raw", tag="wa_then_res", align_bytes=64)
+        wa_raw = keep.tile([P, 2 * R], U8, name="wa_raw", align_bytes=64)
         wb_codes = keep.tile([P, N], U32, name="wb_codes", align_bytes=64)
+        identity = keep.tile([P, P], F32, name="identity")
 
         nc.vector.memset(x_plane[:].bitcast(I32), 0)
         nc.vector.memset(wa_plane_raw[:].bitcast(I32), 0)
-        nc.gpsimd.memset(wb_plane[:].bitcast(I32), 0)
+        nc.vector.memset(wb_plane[:].bitcast(I32), 0)
+        nc.vector.memset(identity[:], 0.0)
+        make_identity(nc, identity[:], nomemset=True)
 
         nc.sync.dma_start(offsets[:], offs)
+        for h in range(2):
+            cols = slice(h * R, (h + 1) * R)
+            nc.sync.dma_start(out=wa_raw[:, cols].bitcast(I32), in_=wa_words[0][:, cols].bitcast(I32))
         load_scale_rows(nc.sync, x_plane, xt_scales)
-        nc.sync.dma_start(out=wa_raw[:].bitcast(I32), in_=wa_words[0].bitcast(I32))
         nc.sync.dma_start(out=x_codes[:].bitcast(I32), in_=xt_words[0].rearrange("p c r -> p (c r)").bitcast(I32))
         load_scale_rows(nc.sync, wa_plane_raw, wa_scales)
+        load_scale_rows(nc.sync, wb_plane, wb_scales)
+        nc.sync.dma_start(out=wb_codes[:].bitcast(I32), in_=wb_words[0].rearrange("p c r -> p (c r)").bitcast(I32))
+        residual = []
+        for n in range(TILES):
+            res_tile = keep.tile([P, T], F32, name=f"res{n}")
+            nc.sync.dma_start(out=res_tile[:], in_=res[n * P : (n + 1) * P, :])
+            residual.append(res_tile)
 
         windows = []
-        for w in range(2):
+        for w in range(3):
             window = keep.tile([P, T], F32, name=f"window{w}")
-            nc.vector.memset(window[:], 0.0)
+            nc.vector.memset(window[:].bitcast(I32), 0)
             windows.append(window)
+        window_of = [windows[0], windows[1], windows[2], windows[0]]
 
         xg_plane = keep.tile([P, J], U8, name="xg_plane", align_bytes=64)
-        xg_codes = keep.tile([P, J], U32, name="xg_codes", align_bytes=64)
         wa_codes = keep.tile([P, 2 * R], U8, name="wa_codes", align_bytes=64)
         wa_plane = keep.tile([P, R], U8, name="wa_plane", align_bytes=64)
+        half = J // 2
 
-        nc.vector.tensor_copy(out=xg_plane[:], in_=x_plane[:].indirect(offsets[:]))
         nc.vector.tensor_copy(
             out=wa_codes[:].bitcast(U16).rearrange("p (t c i) -> p c t i", t=PACK, i=8),
             in_=wa_raw[:].bitcast(U16).rearrange("p (c i t) -> p c t i", t=PACK, i=8),
         )
-        nc.vector.tensor_copy(out=xg_codes[:, :CHUNK], in_=x_codes[:].indirect(offsets[:, : CHUNK // 16]))
+        nc.vector.tensor_copy(out=xg_plane[:], in_=x_plane[:].indirect(offsets[:]))
+        xg_first = keep.tile([P, half], U32, name="xg_first", align_bytes=64)
+        nc.vector.tensor_copy(out=xg_first[:], in_=x_codes[:].indirect(offsets[:, : half // 16]))
         nc.vector.tensor_copy(
             out=wa_plane[:].rearrange("p (t c i) -> p c t i", t=PACK, i=16),
             in_=wa_plane_raw[:].rearrange("p (c i t) -> p c t i", t=PACK, i=16),
         )
-        nc.vector.tensor_copy(out=xg_codes[:, CHUNK:], in_=x_codes[:].indirect(offsets[:, CHUNK // 16 :]))
-
-        residual = []
-        for n in range(TILES):
-            tag = "wa_then_res" if n == 0 else f"res{n}"
-            res_tile = keep.tile([P, T], F32, name=f"res{n}", tag=tag, align_bytes=64)
-            residual.append(res_tile)
-        nc.sync.dma_start(out=residual[0][:], in_=res[0:P, :])
-        nc.sync.dma_start(out=wb_codes[:].bitcast(I32), in_=wb_words[0].rearrange("p c r -> p (c r)").bitcast(I32))
-        load_scale_rows(nc.sync, wb_plane, wb_scales)
-        for n in range(1, TILES):
-            nc.sync.dma_start(out=residual[n][:], in_=res[n * P : (n + 1) * P, :])
+        xg_second = keep.tile([P, half], U32, name="xg_second", tag="plane_then_codes", align_bytes=64)
+        nc.vector.tensor_copy(out=xg_second[:], in_=x_codes[:].indirect(offsets[:, half // 16 :]))
+        xg_codes = [xg_first[:, :CHUNK], xg_first[:, CHUNK:], xg_second[:, :CHUNK], xg_second[:, CHUNK:]]
 
         pre = []
         for c in range(CHUNKS):
-            bank = psum.tile([P, PACK * CHUNK], F32, name=f"pre{c}", tag=f"pre{c}")
-            slots = slice(c * CHUNK, (c + 1) * CHUNK)
+            bank = psum.tile([P, BANK], F32, name=f"pre{c}", tag=f"work{c}")
             for t in range(PACK):
                 nc.tensor.matmul_mx(
                     out=bank[:, t * CHUNK : (t + 1) * CHUNK],
                     lhsT=wa_codes[:, 2 * P * t : 2 * P * (t + 1)].bitcast(FP4X4),
                     lhsT_scale=wa_plane[:, P * t : P * (t + 1)],
-                    rhs=xg_codes[:, slots].bitcast(FP8X4),
-                    rhs_scale=xg_plane[:, slots],
+                    rhs=xg_codes[c].bitcast(FP8X4),
+                    rhs_scale=xg_plane[:, c * CHUNK : (c + 1) * CHUNK],
                     start=True,
                     stop=True,
                 )
@@ -108,7 +116,7 @@ def tile_moe_expert_hidden_less_block_mean_kernel(
 
         groups = PACK * CHUNK // BLOCK
         answers = keep.tile([P, TILES * J], F32, name="answers")
-        sums, hidden = {}, {}
+        sums, hidden, products, turned = {}, {}, {}, {}
 
         def block_sums(c):
             sums[c] = keep.tile([P, groups], F32, name=f"sums{c}")
@@ -137,10 +145,13 @@ def tile_moe_expert_hidden_less_block_mean_kernel(
             codes = keep.tile([P, CHUNK], U32, name=f"hid_codes{c}", align_bytes=64)
             plane = keep.tile([P, CHUNK], U8, name=f"hid_plane{c}", align_bytes=64)
             nc.vector.quantize_mx(out=codes[:].bitcast(FP8X4), scales=plane[:], in_=hidden[c][:])
-            parts = [(0, TILES, f"post{c}")] if c < CHUNKS - 1 else [(0, 1, f"post{c}"), (1, TILES, "pre0")]
-            for first, last, tag in parts:
-                bank = psum.tile([P, PACK * CHUNK], F32, name=f"post{c}_{first}", tag=tag)
-                for n in range(first, last):
+            if c < CHUNKS - 1:
+                parts = [(f"work{c}", [(0, TURNED_TILES), (TURNED_TILES, TILES)])]
+            else:
+                parts = [(f"work{c}", [(0, 1)]), ("work0", [(1, TURNED_TILES), (TURNED_TILES, TILES)])]
+            for tag, copies in parts:
+                bank = psum.tile([P, BANK], F32, name=f"post{c}_{tag}", tag=tag)
+                for n in range(copies[0][0], copies[-1][1]):
                     nc.tensor.matmul_mx(
                         out=bank[:, n * CHUNK : (n + 1) * CHUNK],
                         lhsT=wb_codes[:, n * P : (n + 1) * P].bitcast(FP8X4),
@@ -150,46 +161,96 @@ def tile_moe_expert_hidden_less_block_mean_kernel(
                         start=True,
                         stop=True,
                     )
-                nc.scalar.copy(
+                products.setdefault(c, []).extend((bank, first, last) for first, last in copies)
+
+        def take_answers(c):
+            for bank, first, last in products[c]:
+                nc.scalar.activation(
                     out=answers[:].rearrange("p (n j) -> p n j", n=TILES)[:, first:last, c * CHUNK : (c + 1) * CHUNK],
                     in_=bank[:].rearrange("p (n j) -> p n j", n=TILES)[:, first:last, :],
+                    func=ACT.Copy,
+                    scale=1.0 / RES_SCALE if first < TURNED_TILES else 1.0,
                 )
 
         def scatter(n, first, last):
             nc.vector.tensor_copy(
-                out=windows[n % 2][:].indirect(offsets[:, first // 16 : last // 16]),
+                out=window_of[n][:].indirect(offsets[:, first // 16 : last // 16]),
                 in_=answers[:, n * J + first : n * J + last],
             )
 
-        def finish(n, pieces):
-            width = T // pieces
-            for h in range(pieces):
-                cols = slice(h * width, (h + 1) * width)
-                result = keep.tile([P, width], F32, name=f"result{n}_{h}")
+        def turn(bank, source, first_col, opens, closes):
+            blocks = BANK // P
+            for b in range(blocks):
+                nc.tensor.matmul(
+                    out=bank[:, b * P : (b + 1) * P],
+                    lhsT=source[:, first_col + b * P : first_col + (b + 1) * P],
+                    rhs=identity[:],
+                    is_transpose=True,
+                    start=opens and b == 0,
+                    stop=closes and b == blocks - 1,
+                )
+
+        def turn_residual(n):
+            for h in range(T // BANK):
+                turned[n, h] = psum.tile([P, BANK], F32, name=f"turned{n}_{h}")
+                turn(turned[n, h], residual[n], h * BANK, True, False)
+
+        def add_on_tensor(n, h):
+            turn(turned[n, h], window_of[n], h * BANK, False, True)
+            total = keep.tile([P, BANK], F32, name=f"total{n}_{h}")
+            nc.scalar.activation(out=total[:], in_=turned[n, h][:], func=ACT.Copy, scale=RES_SCALE)
+            return total
+
+        def turn_back(n, h, total, tag):
+            bank = psum.tile([P, BANK], F32, name=f"back{n}_{h}", tag=tag)
+            for b in range(BANK // P):
+                nc.tensor.transpose(bank[:, b * P : (b + 1) * P], total[:, b * P : (b + 1) * P], identity[:])
+            result = keep.tile([P, BANK], F32, name=f"turned_result{n}_{h}")
+            nc.scalar.copy(out=result[:], in_=bank[:])
+            nc.scalar.dma_start(out=out[n * P : (n + 1) * P, h * BANK : (h + 1) * BANK], in_=result[:])
+
+        def add_on_vector(n, widths):
+            first = 0
+            for width in widths:
+                cols = slice(first, first + width)
+                result = keep.tile([P, width], F32, name=f"result{n}_{first}")
                 nc.vector.scalar_tensor_tensor(
-                    out=result[:], in0=residual[n][:, cols], scalar=0.2, in1=windows[n % 2][:, cols], op0=ALU.mult, op1=ALU.add
+                    out=result[:], in0=residual[n][:, cols], scalar=RES_SCALE, in1=window_of[n][:, cols], op0=ALU.mult, op1=ALU.add
                 )
                 nc.sync.dma_start(out=out[n * P : (n + 1) * P, cols], in_=result[:])
+                first = first + width
 
         block_sums(0)
         block_sums(1)
         centre(0)
         block_sums(2)
         centre(1)
-        block_sums(3)
         second_layer(0)
+        block_sums(3)
         centre(2)
+        take_answers(0)
         second_layer(1)
         centre(3)
+        take_answers(1)
+        turn_residual(0)
         second_layer(2)
+        take_answers(2)
+        turn_residual(1)
         scatter(0, 0, 2 * CHUNK)
         second_layer(3)
+        take_answers(3)
         scatter(1, 0, 3 * CHUNK)
         scatter(0, 2 * CHUNK, J)
         scatter(1, 3 * CHUNK, J)
-        finish(0, 1)
-        finish(1, 1)
+        total_00 = add_on_tensor(0, 0)
+        total_01 = add_on_tensor(0, 1)
+        turn_back(0, 0, total_00, "work1")
         scatter(2, 0, J)
+        total_10 = add_on_tensor(1, 0)
+        turn_back(0, 1, total_01, "work2")
+        total_11 = add_on_tensor(1, 1)
         scatter(3, 0, J)
-        finish(2, 1)
-        finish(3, 2)
+        turn_back(1, 0, total_10, "work3")
+        add_on_vector(2, [T])
+        turn_back(1, 1, total_11, "work1")
+        add_on_vector(3, [640, 384])

@@ -24,7 +24,7 @@ CHUNK = 128
 CHUNKS = J // CHUNK
 TILES = N // P
 BANK = 512
-TURNED_TILES = 2
+TURNED_TILES = 1
 RES_SCALE = 0.2
 
 
@@ -73,11 +73,13 @@ def tile_moe_expert_hidden_less_block_mean_kernel(
             residual.append(res_tile)
 
         windows = []
-        for w in range(3):
+        for w in range(2):
             window = keep.tile([P, T], F32, name=f"window{w}")
             nc.vector.memset(window[:].bitcast(I32), 0)
             windows.append(window)
-        window_of = [windows[0], windows[1], windows[2], windows[0]]
+        warm = keep.tile([P, 1], F32, name="warm")
+        nc.scalar.activation(out=warm[:], in_=windows[0][:, 0:1], func=ACT.Relu)
+        window_of = [windows[0], windows[1], windows[1], windows[0]]
 
         xg_plane = keep.tile([P, J], U8, name="xg_plane", align_bytes=64)
         wa_codes = keep.tile([P, 2 * R], U8, name="wa_codes", align_bytes=64)
@@ -146,12 +148,12 @@ def tile_moe_expert_hidden_less_block_mean_kernel(
             plane = keep.tile([P, CHUNK], U8, name=f"hid_plane{c}", align_bytes=64)
             nc.vector.quantize_mx(out=codes[:].bitcast(FP8X4), scales=plane[:], in_=hidden[c][:])
             if c < CHUNKS - 1:
-                parts = [(f"work{c}", [(0, TURNED_TILES), (TURNED_TILES, TILES)])]
+                parts = [(f"work{c}", [0, 1, 2, 3])]
             else:
-                parts = [(f"work{c}", [(0, 1)]), ("work0", [(1, TURNED_TILES), (TURNED_TILES, TILES)])]
-            for tag, copies in parts:
+                parts = [("last_first", [1]), ("last_rest", [0, 2, 3])]
+            for tag, tiles in parts:
                 bank = psum.tile([P, BANK], F32, name=f"post{c}_{tag}", tag=tag)
-                for n in range(copies[0][0], copies[-1][1]):
+                for n in tiles:
                     nc.tensor.matmul_mx(
                         out=bank[:, n * CHUNK : (n + 1) * CHUNK],
                         lhsT=wb_codes[:, n * P : (n + 1) * P].bitcast(FP8X4),
@@ -161,16 +163,15 @@ def tile_moe_expert_hidden_less_block_mean_kernel(
                         start=True,
                         stop=True,
                     )
-                products.setdefault(c, []).extend((bank, first, last) for first, last in copies)
+                    products[c, n] = bank
 
-        def take_answers(c):
-            for bank, first, last in products[c]:
-                nc.scalar.activation(
-                    out=answers[:].rearrange("p (n j) -> p n j", n=TILES)[:, first:last, c * CHUNK : (c + 1) * CHUNK],
-                    in_=bank[:].rearrange("p (n j) -> p n j", n=TILES)[:, first:last, :],
-                    func=ACT.Copy,
-                    scale=1.0 / RES_SCALE if first < TURNED_TILES else 1.0,
-                )
+        def take_answers(c, first, last):
+            nc.scalar.activation(
+                out=answers[:].rearrange("p (n j) -> p n j", n=TILES)[:, first:last, c * CHUNK : (c + 1) * CHUNK],
+                in_=products[c, first][:].rearrange("p (n j) -> p n j", n=TILES)[:, first:last, :],
+                func=ACT.Copy,
+                scale=1.0 / RES_SCALE if first < TURNED_TILES else 1.0,
+            )
 
         def scatter(n, first, last):
             nc.vector.tensor_copy(
@@ -209,16 +210,17 @@ def tile_moe_expert_hidden_less_block_mean_kernel(
             nc.scalar.copy(out=result[:], in_=bank[:])
             nc.scalar.dma_start(out=out[n * P : (n + 1) * P, h * BANK : (h + 1) * BANK], in_=result[:])
 
-        def add_on_vector(n, widths):
-            first = 0
-            for width in widths:
-                cols = slice(first, first + width)
-                result = keep.tile([P, width], F32, name=f"result{n}_{first}")
-                nc.vector.scalar_tensor_tensor(
-                    out=result[:], in0=residual[n][:, cols], scalar=RES_SCALE, in1=window_of[n][:, cols], op0=ALU.mult, op1=ALU.add
-                )
-                nc.sync.dma_start(out=out[n * P : (n + 1) * P, cols], in_=result[:])
-                first = first + width
+        def add_on_vector(n, first, last):
+            result = keep.tile([P, last - first], F32, name=f"result{n}_{first}")
+            nc.vector.scalar_tensor_tensor(
+                out=result[:],
+                in0=residual[n][:, first:last],
+                scalar=RES_SCALE,
+                in1=window_of[n][:, first:last],
+                op0=ALU.mult,
+                op1=ALU.add,
+            )
+            nc.sync.dma_start(out=out[n * P : (n + 1) * P, first:last], in_=result[:])
 
         block_sums(0)
         block_sums(1)
@@ -228,29 +230,36 @@ def tile_moe_expert_hidden_less_block_mean_kernel(
         second_layer(0)
         block_sums(3)
         centre(2)
-        take_answers(0)
+        take_answers(0, 1, TILES)
+        take_answers(0, 0, 1)
         second_layer(1)
         centre(3)
-        take_answers(1)
+        take_answers(1, 1, 2)
+        take_answers(1, 0, 1)
         turn_residual(0)
         second_layer(2)
-        take_answers(2)
-        turn_residual(1)
-        scatter(0, 0, 2 * CHUNK)
+        take_answers(2, 0, 1)
+        take_answers(2, 1, 2)
+        scatter(1, 0, 2 * CHUNK)
         second_layer(3)
-        take_answers(3)
-        scatter(1, 0, 3 * CHUNK)
-        scatter(0, 2 * CHUNK, J)
-        scatter(1, 3 * CHUNK, J)
-        total_00 = add_on_tensor(0, 0)
-        total_01 = add_on_tensor(0, 1)
-        turn_back(0, 0, total_00, "work1")
+        take_answers(3, 1, 2)
+        take_answers(3, 0, 1)
+        scatter(0, 0, 3 * CHUNK)
+        scatter(1, 2 * CHUNK, J)
+        scatter(0, 3 * CHUNK, J)
+        for c in range(1, CHUNKS):
+            take_answers(c, 2, TILES)
+        total_0 = add_on_tensor(0, 0)
+        total_1 = add_on_tensor(0, 1)
+        turn_back(0, 0, total_0, "work0")
+        turn_back(0, 1, total_1, "work3")
+        add_on_vector(1, 0, BANK)
+        add_on_vector(1, BANK, T)
         scatter(2, 0, J)
-        total_10 = add_on_tensor(1, 0)
-        turn_back(0, 1, total_01, "work2")
-        total_11 = add_on_tensor(1, 1)
-        scatter(3, 0, J)
-        turn_back(1, 0, total_10, "work3")
-        add_on_vector(2, [T])
-        turn_back(1, 1, total_11, "work1")
-        add_on_vector(3, [640, 384])
+        scatter(3, 0, J // 2)
+        add_on_vector(2, 0, BANK)
+        scatter(3, J // 2, J)
+        add_on_vector(2, BANK, T)
+        add_on_vector(3, 0, 384)
+        add_on_vector(3, 384, 768)
+        add_on_vector(3, 768, T)

from contextlib import ExitStack

import concourse.mybir as mybir
from concourse.masks import make_identity

K, T, J, R, N = 512, 1024, 512, 512, 512
FLOPS = 2 * K * R * J + 2 * R * N * J

F32 = mybir.dt.float32
BF16 = mybir.dt.bfloat16
I32 = mybir.dt.int32
U32 = mybir.dt.uint32
U16 = mybir.dt.uint16
U8 = mybir.dt.uint8
FP8X4 = mybir.dt.float8_e4m3fn_x4
FP4X4 = mybir.dt.float4_e2m1fn_x4
ALU = mybir.AluOpType
ACT = mybir.ActivationFunctionType

P = 128
PACK = 4
BLOCK = 8
CHUNK = 128
CHUNKS = J // CHUNK
TILES = N // P
BANK = 512
TURNED_TILES = 1
RES_SCALE = 0.2


def load_scale_rows(engine, plane, scales):
    rows = scales[0].bitcast(I32).rearrange("(q r) c -> r q c", r=4)
    for r in range(4):
        engine.dma_start(out=plane[r:P:32, :].bitcast(I32), in_=rows[r])


def tile_moe_expert_hidden_less_block_mean_kernel(
    tc, xt_words, xt_scales, wa_words, wa_scales, wb_words, wb_scales, res, offs, out
):
    nc = tc.nc
    with ExitStack() as ctx:
        keep = ctx.enter_context(tc.tile_pool(name="keep", bufs=1))
        psum = ctx.enter_context(tc.psum_pool(name="psum", bufs=1))

        offsets = keep.tile([P, J // 16], U16, name="offsets")
        x_plane = keep.tile([P, T], U8, name="x_plane", align_bytes=64)
        wa_plane_raw = keep.tile([P, R], U8, name="wa_plane_raw", tag="plane_then_codes", align_bytes=64)
        wb_plane = keep.tile([P, N], U8, name="wb_plane", align_bytes=64)
        x_codes = keep.tile([P, T], U32, name="x_codes", align_bytes=64)
        wa_raw = keep.tile([P, 2 * R], U8, name="wa_raw", align_bytes=64)
        wb_codes = keep.tile([P, N], U32, name="wb_codes", align_bytes=64)
        identity = keep.tile([P, P], F32, name="identity")

        nc.vector.memset(x_plane[:].bitcast(I32), 0)
        nc.vector.memset(wa_plane_raw[:].bitcast(I32), 0)
        nc.vector.memset(wb_plane[:].bitcast(I32), 0)
        nc.vector.memset(identity[:], 0.0)
        make_identity(nc, identity[:], nomemset=True)

        nc.sync.dma_start(offsets[:], offs)
        for h in range(2):
            cols = slice(h * R, (h + 1) * R)
            nc.sync.dma_start(out=wa_raw[:, cols].bitcast(I32), in_=wa_words[0][:, cols].bitcast(I32))
        load_scale_rows(nc.sync, x_plane, xt_scales)
        nc.sync.dma_start(out=x_codes[:].bitcast(I32), in_=xt_words[0].rearrange("p c r -> p (c r)").bitcast(I32))
        load_scale_rows(nc.sync, wa_plane_raw, wa_scales)
        load_scale_rows(nc.sync, wb_plane, wb_scales)
        nc.sync.dma_start(out=wb_codes[:].bitcast(I32), in_=wb_words[0].rearrange("p c r -> p (c r)").bitcast(I32))
        residual = []
        for n in range(TILES):
            res_tile = keep.tile([P, T], F32, name=f"res{n}")
            nc.sync.dma_start(out=res_tile[:], in_=res[n * P : (n + 1) * P, :])
            residual.append(res_tile)

        windows = []
        for w in range(2):
            window = keep.tile([P, T], F32, name=f"window{w}")
            nc.vector.memset(window[:].bitcast(I32), 0)
            windows.append(window)
        warm = keep.tile([P, 1], F32, name="warm")
        nc.scalar.activation(out=warm[:], in_=windows[0][:, 0:1], func=ACT.Relu)
        window_of = [windows[0], windows[1], windows[1], windows[0]]

        xg_plane = keep.tile([P, J], U8, name="xg_plane", align_bytes=64)
        wa_codes = keep.tile([P, 2 * R], U8, name="wa_codes", align_bytes=64)
        wa_plane = keep.tile([P, R], U8, name="wa_plane", align_bytes=64)
        half = J // 2

        nc.vector.tensor_copy(
            out=wa_codes[:].bitcast(U16).rearrange("p (t c i) -> p c t i", t=PACK, i=8),
            in_=wa_raw[:].bitcast(U16).rearrange("p (c i t) -> p c t i", t=PACK, i=8),
        )
        nc.vector.tensor_copy(out=xg_plane[:], in_=x_plane[:].indirect(offsets[:]))
        xg_first = keep.tile([P, half], U32, name="xg_first", align_bytes=64)
        nc.vector.tensor_copy(out=xg_first[:], in_=x_codes[:].indirect(offsets[:, : half // 16]))
        nc.vector.tensor_copy(
            out=wa_plane[:].rearrange("p (t c i) -> p c t i", t=PACK, i=16),
            in_=wa_plane_raw[:].rearrange("p (c i t) -> p c t i", t=PACK, i=16),
        )
        xg_second = keep.tile([P, half], U32, name="xg_second", tag="plane_then_codes", align_bytes=64)
        nc.vector.tensor_copy(out=xg_second[:], in_=x_codes[:].indirect(offsets[:, half // 16 :]))
        xg_codes = [xg_first[:, :CHUNK], xg_first[:, CHUNK:], xg_second[:, :CHUNK], xg_second[:, CHUNK:]]

        pre = []
        for c in range(CHUNKS):
            bank = psum.tile([P, BANK], F32, name=f"pre{c}", tag=f"work{c}")
            for t in range(PACK):
                nc.tensor.matmul_mx(
                    out=bank[:, t * CHUNK : (t + 1) * CHUNK],
                    lhsT=wa_codes[:, 2 * P * t : 2 * P * (t + 1)].bitcast(FP4X4),
                    lhsT_scale=wa_plane[:, P * t : P * (t + 1)],
                    rhs=xg_codes[c].bitcast(FP8X4),
                    rhs_scale=xg_plane[:, c * CHUNK : (c + 1) * CHUNK],
                    start=True,
                    stop=True,
                )
            pre.append(bank)

        groups = PACK * CHUNK // BLOCK
        answers = keep.tile([P, TILES * J], F32, name="answers")
        sums, hidden, products, turned = {}, {}, {}, {}

        def block_sums(c):
            sums[c] = keep.tile([P, groups], F32, name=f"sums{c}")
            nc.vector.tensor_reduce(
                out=sums[c][:], in_=pre[c][:].rearrange("p (g i) -> p g i", i=BLOCK), axis=mybir.AxisListType.X, op=ALU.add
            )

        def centre(c):
            centred = keep.tile([P, PACK * CHUNK], F32, name=f"centred{c}")
            nc.vector.scalar_tensor_tensor(
                out=centred[:].rearrange("p (g i) -> p g i", i=BLOCK),
                in0=sums[c][:].unsqueeze(2).to_broadcast([P, groups, BLOCK]),
                scalar=-1.0 / BLOCK,
                in1=pre[c][:].rearrange("p (g i) -> p g i", i=BLOCK),
                op0=ALU.mult,
                op1=ALU.add,
            )
            hidden[c] = keep.tile([P, CHUNK * PACK], BF16, name=f"hidden{c}", align_bytes=64)
            nc.scalar.activation(
                out=hidden[c][:].rearrange("p (c i t) -> p c t i", t=PACK, i=4),
                in_=centred[:].rearrange("p (t c i) -> p c t i", t=PACK, i=4),
                func=ACT.Relu,
            )

        def second_layer(c):
            codes = keep.tile([P, CHUNK], U32, name=f"hid_codes{c}", align_bytes=64)
            plane = keep.tile([P, CHUNK], U8, name=f"hid_plane{c}", align_bytes=64)
            nc.vector.quantize_mx(out=codes[:].bitcast(FP8X4), scales=plane[:], in_=hidden[c][:])
            if c < CHUNKS - 1:
                parts = [(f"work{c}", [0, 1, 2, 3])]
            else:
                parts = [("last_first", [1]), ("last_rest", [0, 2, 3])]
            for tag, tiles in parts:
                bank = psum.tile([P, BANK], F32, name=f"post{c}_{tag}", tag=tag)
                for n in tiles:
                    nc.tensor.matmul_mx(
                        out=bank[:, n * CHUNK : (n + 1) * CHUNK],
                        lhsT=wb_codes[:, n * P : (n + 1) * P].bitcast(FP8X4),
                        lhsT_scale=wb_plane[:, n * P : (n + 1) * P],
                        rhs=codes[:].bitcast(FP8X4),
                        rhs_scale=plane[:],
                        start=True,
                        stop=True,
                    )
                    products[c, n] = bank

        def take_answers(c, first, last):
            nc.scalar.activation(
                out=answers[:].rearrange("p (n j) -> p n j", n=TILES)[:, first:last, c * CHUNK : (c + 1) * CHUNK],
                in_=products[c, first][:].rearrange("p (n j) -> p n j", n=TILES)[:, first:last, :],
                func=ACT.Copy,
                scale=1.0 / RES_SCALE if first < TURNED_TILES else 1.0,
            )

        def scatter(n, first, last):
            nc.vector.tensor_copy(
                out=window_of[n][:].indirect(offsets[:, first // 16 : last // 16]),
                in_=answers[:, n * J + first : n * J + last],
            )

        def turn(bank, source, first_col, opens, closes):
            blocks = BANK // P
            for b in range(blocks):
                nc.tensor.matmul(
                    out=bank[:, b * P : (b + 1) * P],
                    lhsT=source[:, first_col + b * P : first_col + (b + 1) * P],
                    rhs=identity[:],
                    is_transpose=True,
                    start=opens and b == 0,
                    stop=closes and b == blocks - 1,
                )

        def turn_residual(n):
            for h in range(T // BANK):
                turned[n, h] = psum.tile([P, BANK], F32, name=f"turned{n}_{h}")
                turn(turned[n, h], residual[n], h * BANK, True, False)

        def add_on_tensor(n, h):
            turn(turned[n, h], window_of[n], h * BANK, False, True)
            total = keep.tile([P, BANK], F32, name=f"total{n}_{h}")
            nc.scalar.activation(out=total[:], in_=turned[n, h][:], func=ACT.Copy, scale=RES_SCALE)
            return total

        def turn_back(n, h, total, tag):
            bank = psum.tile([P, BANK], F32, name=f"back{n}_{h}", tag=tag)
            for b in range(BANK // P):
                nc.tensor.transpose(bank[:, b * P : (b + 1) * P], total[:, b * P : (b + 1) * P], identity[:])
            result = keep.tile([P, BANK], F32, name=f"turned_result{n}_{h}")
            nc.scalar.copy(out=result[:], in_=bank[:])
            nc.scalar.dma_start(out=out[n * P : (n + 1) * P, h * BANK : (h + 1) * BANK], in_=result[:])

        def add_on_vector(n, first, last):
            result = keep.tile([P, last - first], F32, name=f"result{n}_{first}")
            nc.vector.scalar_tensor_tensor(
                out=result[:],
                in0=residual[n][:, first:last],
                scalar=RES_SCALE,
                in1=window_of[n][:, first:last],
                op0=ALU.mult,
                op1=ALU.add,
            )
            nc.sync.dma_start(out=out[n * P : (n + 1) * P, first:last], in_=result[:])

        block_sums(0)
        block_sums(1)
        centre(0)
        block_sums(2)
        centre(1)
        second_layer(0)
        block_sums(3)
        centre(2)
        take_answers(0, 1, TILES)
        take_answers(0, 0, 1)
        second_layer(1)
        centre(3)
        take_answers(1, 1, 2)
        take_answers(1, 0, 1)
        turn_residual(0)
        second_layer(2)
        take_answers(2, 0, 1)
        take_answers(2, 1, 2)
        scatter(1, 0, 2 * CHUNK)
        second_layer(3)
        take_answers(3, 1, 2)
        take_answers(3, 0, 1)
        scatter(0, 0, 3 * CHUNK)
        scatter(1, 2 * CHUNK, J)
        scatter(0, 3 * CHUNK, J)
        for c in range(1, CHUNKS):
            take_answers(c, 2, TILES)
        total_0 = add_on_tensor(0, 0)
        total_1 = add_on_tensor(0, 1)
        turn_back(0, 0, total_0, "work0")
        turn_back(0, 1, total_1, "work3")
        add_on_vector(1, 0, BANK)
        add_on_vector(1, BANK, T)
        scatter(2, 0, J)
        scatter(3, 0, J // 2)
        add_on_vector(2, 0, BANK)
        scatter(3, J // 2, J)
        add_on_vector(2, BANK, T)
        add_on_vector(3, 0, 384)
        add_on_vector(3, 384, 768)
        add_on_vector(3, 768, T)
